import numpy as np
import ml_dtypes


def mxq(x, axis, fmt="e4m3"):
    dtype, down = {"e4m3": (ml_dtypes.float8_e4m3fn, 7), "e5m2": (ml_dtypes.float8_e5m2, 14)}[fmt]
    v = np.moveaxis(np.asarray(x, np.float32).astype(ml_dtypes.bfloat16).astype(np.float64), axis, -1)
    blocks = v.reshape(v.shape[:-1] + (-1, 32))
    amax = np.abs(blocks).max(-1, keepdims=True)
    byte = np.maximum(np.where(amax > 0, np.frexp(amax)[1] - 1 + 127, 0) - down, 1)
    scale = np.exp2(byte - 127.0)
    codes = (blocks / scale).astype(np.float32).astype(dtype).astype(np.float64)
    return np.moveaxis((codes * scale).reshape(v.shape), -1, axis)


WIDE = False


def mx_kscale(k):
    if not WIDE:
        return np.ones(k)
    levels = np.array([10, -10, 5, -5, 0])
    if k % 512:
        return np.exp2(np.random.permutation(np.resize(levels, k // 32))).repeat(32)
    a = np.empty((k // 512, 16))
    for p in range(k // 512):
        a[p, :8] = np.random.permutation(np.resize(levels, 8))
        for g in range(8):
            far = levels[np.abs(levels - a[p, g]) >= 10]
            a[p, g + 8] = far[np.random.randint(len(far))]
    return np.exp2(a.ravel()).repeat(32)


def f64(x):
    return np.asarray(x).astype(np.float64)


def striped(idx):
    return np.tile(np.asarray(idx).reshape(-1, 16).T, (8, 1)).astype(np.uint16)


def unstriped(offs):
    return offs[:16].T.reshape(-1).astype(np.int64)


B, N, T, D, DV, NQ = 1, 1024, 4096, 512, 256, 128
PAGE = 128
CAP = 2.0


def setup_inputs():
    n = np.random.standard_normal
    pages = np.random.permutation(T // PAGE)[:B * N // PAGE]
    idx = (pages[:, None] * PAGE + np.arange(PAGE)[None, :]).reshape(-1)
    s = mx_kscale(D)[:, None]
    u = np.ones(T)
    u[idx] = mx_kscale(B * N)
    r = np.random.uniform(0.5, 2.0, T)
    k = n((D, T)) / s
    v = n((DV, T)) / (u * r)
    return {
        "qT": (n((B, D, NQ)) * s * (1.00 / np.sqrt(D))).astype(np.float32),
        "kT": k.astype(np.float32),
        "vT": v.astype(np.float32),
        "vs": np.tile(u * r, (128, 1)).astype(np.float32),
        "sink": (2.0 + 3.0 * n((B, NQ, 1))).astype(np.float32),
        "offs": striped(idx),
    }


def reference(qT, kT, vT, vs, sink, offs):
    idx = unstriped(offs)
    k = f64(kT)
    v = f64(vT)
    pick = lambda x: x[:, idx].reshape(x.shape[0], B, N).transpose(1, 0, 2)
    q = f64(qT)
    score = mxq(q, 1, "e4m3").transpose(0, 2, 1) @ mxq(pick(k), 1, "e4m3")
    score = CAP * np.tanh(score / CAP)
    m = np.maximum(score.max(-1, keepdims=True), f64(sink))
    p = np.exp(score - m)
    total = p.sum(-1, keepdims=True) + np.exp(f64(sink) - m)
    w = p * pick(f64(vs))[:, :1, :]
    y = mxq(w, 2, "e4m3") @ mxq(pick(v).transpose(0, 2, 1), 1, "e4m3")
    y = y / total
    return y

@@ -1,0 +1,195 @@
+import concourse.mybir as mybir
+from concourse.masks import make_identity
+
+NQ, D, DV, T, N = 128, 512, 256, 4096, 1024
+P = 128
+PACK = 4
+PASS = P * PACK
+PASSES = N // PASS
+EB = DV // P
+
+FLOPS = 2 * NQ * N * (D + DV)
+BYTES = 4 * (D * T + DV * T + D * NQ + T + NQ + NQ * DV) + 2 * P * (N // 16)
+
+F32 = mybir.dt.float32
+BF16 = mybir.dt.bfloat16
+U32 = mybir.dt.uint32
+U16 = mybir.dt.uint16
+U8 = mybir.dt.uint8
+FP8X4 = mybir.dt.float8_e4m3fn_x4
+ACT = mybir.ActivationFunctionType
+ALU = mybir.AluOpType
+
+
+def tile_attend_x_cap_sink_kernel(tc, qT, kT, vT, vs, sink, offs, out):
+    nc = tc.nc
+    with (
+        tc.tile_pool(name="held", bufs=1) as held,
+        tc.psum_pool(name="turned", bufs=4) as turned_pool,
+        tc.psum_pool(name="sums", bufs=1) as sums_pool,
+    ):
+        offsets = held.tile([P, N // 16], U16, name="offsets")
+        nc.sync.dma_start(offsets[:], offs)
+
+        tiny = held.tile([P, 1], F32, name="tiny")
+        nc.vector.memset(tiny[:], 0.0)
+        tiny_out = held.tile([P, 1], F32, name="tiny_out")
+        nc.scalar.activation(tiny_out[:], tiny[:], ACT.Exp)
+
+        vs_pool = held.tile([P, T], F32, name="vs_pool")
+        nc.vector.memset(vs_pool[:], 0.0)
+        sink_row = held.tile([P, P], F32, name="sink_row")
+        nc.vector.memset(sink_row[:], 0.0)
+        ident = held.tile([P, P], F32, name="ident")
+        make_identity(nc, ident[:])
+
+        k_rows = kT.rearrange("(p j) t -> p j t", j=PACK)
+        k_pool = [held.tile([P, T], F32, name=f"k_pool{j}") for j in range(PACK)]
+        v_pool = [held.tile([P, T], F32, name=f"v_pool{b}") for b in range(EB)]
+        q_raw = held.tile([P, PACK, NQ], F32, name="q_raw")
+
+        nc.sync.dma_start(k_pool[0][:], k_rows[:, 0, :])
+        nc.sync.dma_start(q_raw[:], qT[0].rearrange("(p j) w -> p j w", j=PACK))
+        nc.sync.dma_start(sink_row[0:1, :], sink[0].rearrange("q o -> o q"))
+        nc.sync.dma_start(vs_pool[0:1, :], vs[0:1, :])
+        for j in range(1, PACK):
+            nc.sync.dma_start(k_pool[j][:], k_rows[:, j, :])
+        for b in range(EB):
+            nc.sync.dma_start(v_pool[b][:], vT[b * P : (b + 1) * P, :])
+
+        q_grouped = held.tile([P, NQ, PACK], BF16, align_bytes=64, name="q_grouped")
+        q_codes = held.tile([P, NQ], U32, align_bytes=64, name="q_codes")
+        q_scales = held.tile([P, NQ], U8, align_bytes=64, name="q_scales")
+
+        k_picked = held.tile([P, PACK, N], F32, name="k_picked")
+        nc.vector.tensor_copy(k_picked[:, 0, :], k_pool[0][:].indirect(offsets[:]))
+        nc.scalar.copy(q_grouped[:], q_raw[:].rearrange("p j w -> p w j"))
+        nc.vector.quantize_mx(
+            out=q_codes[:].bitcast(FP8X4), scales=q_scales[:], in_=q_grouped[:].rearrange("p w j -> p (w j)")
+        )
+
+        sink_turned = turned_pool.tile([P, PACK, P], F32, tag="turned", name="sink_turned")
+        nc.tensor.transpose(sink_turned[:, 0, :], sink_row[:], ident[:])
+        neg_sink = held.tile([P, 1], F32, name="neg_sink")
+        sink_col = held.tile([P, 1], F32, name="sink_col")
+        nc.vector.tensor_scalar(neg_sink[:], sink_turned[:, 0, 0:1], -1.0, None, ALU.mult)
+        nc.vector.tensor_scalar(sink_col[:], neg_sink[:], -1.0, None, ALU.mult)
+
+        vs_picked = held.tile([P, N], F32, name="vs_picked")
+        nc.vector.tensor_copy(vs_picked[:], vs_pool[:].indirect(offsets[:]))
+        vs_cols = held.tile([P, PASSES, PACK], F32, name="vs_cols")
+        for g in range(PASSES):
+            vs_turned = turned_pool.tile([P, PACK, P], F32, tag="turned", name="vs_turned")
+            for t in range(PACK):
+                nc.tensor.transpose(
+                    vs_turned[:, t, :], vs_picked[:, g * PASS + t : (g + 1) * PASS : PACK], ident[:]
+                )
+            nc.scalar.copy(vs_cols[:, g, :], vs_turned[:, :, 0])
+
+        for j in range(1, PACK - 1):
+            nc.vector.tensor_copy(k_picked[:, j, :], k_pool[j][:].indirect(offsets[:]))
+
+        half_cols = PASS // 16
+        last = PACK - 1
+        for h in range(PASSES):
+            nc.vector.tensor_copy(
+                k_picked[:, last, h * PASS : (h + 1) * PASS],
+                k_pool[last][:].indirect(offsets[:, h * half_cols : (h + 1) * half_cols]),
+            )
+        k_grouped = [held.tile([P, PASS, PACK], BF16, align_bytes=64, name=f"k_grouped{h}") for h in range(PASSES)]
+        k_codes = [held.tile([P, PASS], U32, align_bytes=64, name=f"k_codes{h}") for h in range(PASSES)]
+        k_scales = [held.tile([P, PASS], U8, align_bytes=64, name=f"k_scales{h}") for h in range(PASSES)]
+        nc.scalar.copy(k_grouped[0][:], k_picked[:, :, 0:PASS].rearrange("p j s -> p s j"))
+        nc.vector.tensor_copy(k_grouped[1][:], k_picked[:, :, PASS:N].rearrange("p j s -> p s j"))
+
+        score = [sums_pool.tile([NQ, PASS], F32, name=f"score{h}") for h in range(PASSES)]
+        capped = held.tile([NQ, N], F32, name="capped")
+        minus_capped = held.tile([NQ, N], F32, name="minus_capped")
+        order = (1, 0)
+        neg_max = [held.tile([NQ, 1], F32, name=f"neg_max{i}") for i in range(PASSES)]
+        before = neg_sink
+        for i, h in enumerate(order):
+            cols = slice(h * PASS, (h + 1) * PASS)
+            nc.vector.quantize_mx(
+                out=k_codes[h][:].bitcast(FP8X4), scales=k_scales[h][:], in_=k_grouped[h][:].rearrange("p s j -> p (s j)")
+            )
+            nc.tensor.matmul_mx(
+                out=score[h][:],
+                lhsT=q_codes[:].bitcast(FP8X4),
+                lhsT_scale=q_scales[:],
+                rhs=k_codes[h][:].bitcast(FP8X4),
+                rhs_scale=k_scales[h][:],
+                start=True,
+                stop=True,
+            )
+            nc.scalar.activation(capped[:, cols], score[h][:], ACT.Tanh, scale=0.5)
+            nc.vector.tensor_scalar(
+                minus_capped[:, cols], capped[:, cols], -2.0, before[:], ALU.mult, ALU.min, accum_out=neg_max[i][:]
+            )
+            before = neg_max[i]
+
+        p = held.tile([NQ, N], F32, name="p")
+        p_sum = [held.tile([NQ, 1], F32, name=f"p_sum{g}") for g in range(PASSES)]
+        w_codes = [held.tile([P, NQ], U32, align_bytes=64, name=f"w_codes{g}") for g in range(PASSES)]
+        w_scales = [held.tile([P, NQ], U8, align_bytes=64, name=f"w_scales{g}") for g in range(PASSES)]
+        for g in range(PASSES):
+            cols = slice(g * PASS, (g + 1) * PASS)
+            nc.scalar.activation(
+                p[:, cols], minus_capped[:, cols], ACT.Exp, bias=before[:], scale=-1.0, accum_out=p_sum[g][:]
+            )
+            p_turned = turned_pool.tile([P, PACK, P], F32, tag="turned", name="p_turned")
+            for t in range(PACK):
+                nc.tensor.transpose(p_turned[:, t, :], p[:, g * PASS + t : (g + 1) * PASS : PACK], ident[:])
+            w_grouped = held.tile([P, NQ, PACK], BF16, align_bytes=64, name=f"w_grouped{g}")
+            nc.vector.tensor_tensor(
+                w_grouped[:],
+                p_turned[:].rearrange("p j q -> p q j"),
+                vs_cols[:, g, :].unsqueeze(1).to_broadcast([P, NQ, PACK]),
+                ALU.mult,
+            )
+            nc.vector.quantize_mx(
+                out=w_codes[g][:].bitcast(FP8X4), scales=w_scales[g][:], in_=w_grouped[:].rearrange("p q j -> p (q j)")
+            )
+
+        sink_term = held.tile([NQ, 1], F32, name="sink_term")
+        nc.scalar.activation(sink_term[:], sink_col[:], ACT.Exp, bias=before[:])
+        total0 = held.tile([NQ, 1], F32, name="total0")
+        total = held.tile([NQ, 1], F32, name="total")
+        recip = held.tile([NQ, 1], F32, name="recip")
+        nc.vector.tensor_tensor(total0[:], p_sum[0][:], p_sum[1][:], ALU.add)
+        nc.vector.tensor_tensor(total[:], total0[:], sink_term[:], ALU.add)
+        nc.vector.reciprocal(recip[:], total[:])
+
+        for b in range(EB):
+            v_picked = held.tile([P, N], F32, name=f"v_picked{b}")
+            y = sums_pool.tile([NQ, P], F32, name=f"y{b}")
+            for g in range(PASSES):
+                nc.vector.tensor_copy(
+                    v_picked[:, g * PASS : (g + 1) * PASS],
+                    v_pool[b][:].indirect(offsets[:, g * half_cols : (g + 1) * half_cols]),
+                )
+            for g in range(PASSES):
+                v_turned = turned_pool.tile([P, PACK, P], F32, tag="turned", name="v_turned")
+                for t in range(PACK):
+                    nc.tensor.transpose(
+                        v_turned[:, t, :], v_picked[:, g * PASS + t : (g + 1) * PASS : PACK], ident[:]
+                    )
+                v_grouped = held.tile([P, P, PACK], BF16, align_bytes=64, name=f"v_grouped{b}{g}")
+                v_codes = held.tile([P, P], U32, align_bytes=64, name=f"v_codes{b}{g}")
+                v_scales = held.tile([P, P], U8, align_bytes=64, name=f"v_scales{b}{g}")
+                nc.scalar.copy(v_grouped[:], v_turned[:].rearrange("p j e -> p e j"))
+                nc.vector.quantize_mx(
+                    out=v_codes[:].bitcast(FP8X4), scales=v_scales[:], in_=v_grouped[:].rearrange("p e j -> p (e j)")
+                )
+                nc.tensor.matmul_mx(
+                    out=y[:],
+                    lhsT=w_codes[g][:].bitcast(FP8X4),
+                    lhsT_scale=w_scales[g][:],
+                    rhs=v_codes[:].bitcast(FP8X4),
+                    rhs_scale=v_scales[:],
+                    start=(g == 0),
+                    stop=(g == PASSES - 1),
+                )
+            y_out = held.tile([NQ, P], F32, name=f"y_out{b}")
+            nc.vector.tensor_scalar(y_out[:], y[:], recip[:], None, ALU.mult)
+            nc.sync.dma_start(out[0, :, b * P : (b + 1) * P], y_out[:])

@@ -61,8 +61,8 @@ def tile_attend_x_cap_sink_kernel(tc, qT, kT, vT, vs, sink, offs, out):
         q_codes = held.tile([P, NQ], U32, align_bytes=64, name="q_codes")
         q_scales = held.tile([P, NQ], U8, align_bytes=64, name="q_scales")
 
-        k_picked = held.tile([P, PACK, N], F32, name="k_picked")
-        nc.vector.tensor_copy(k_picked[:, 0, :], k_pool[0][:].indirect(offsets[:]))
+        k_grouped = held.tile([P, N, PACK], BF16, align_bytes=64, name="k_grouped")
+        nc.vector.tensor_copy(k_grouped[:, :, 0], k_pool[0][:].indirect(offsets[:]))
         nc.scalar.copy(q_grouped[:], q_raw[:].rearrange("p j w -> p w j"))
         nc.vector.quantize_mx(
             out=q_codes[:].bitcast(FP8X4), scales=q_scales[:], in_=q_grouped[:].rearrange("p w j -> p (w j)")
@@ -87,31 +87,26 @@ def tile_attend_x_cap_sink_kernel(tc, qT, kT, vT, vs, sink, offs, out):
             nc.scalar.copy(vs_cols[:, g, :], vs_turned[:, :, 0])
 
         for j in range(1, PACK - 1):
-            nc.vector.tensor_copy(k_picked[:, j, :], k_pool[j][:].indirect(offsets[:]))
+            nc.vector.tensor_copy(k_grouped[:, :, j], k_pool[j][:].indirect(offsets[:]))
 
         half_cols = PASS // 16
         last = PACK - 1
-        for h in range(PASSES):
-            nc.vector.tensor_copy(
-                k_picked[:, last, h * PASS : (h + 1) * PASS],
-                k_pool[last][:].indirect(offsets[:, h * half_cols : (h + 1) * half_cols]),
-            )
-        k_grouped = [held.tile([P, PASS, PACK], BF16, align_bytes=64, name=f"k_grouped{h}") for h in range(PASSES)]
         k_codes = [held.tile([P, PASS], U32, align_bytes=64, name=f"k_codes{h}") for h in range(PASSES)]
         k_scales = [held.tile([P, PASS], U8, align_bytes=64, name=f"k_scales{h}") for h in range(PASSES)]
-        nc.scalar.copy(k_grouped[0][:], k_picked[:, :, 0:PASS].rearrange("p j s -> p s j"))
-        nc.vector.tensor_copy(k_grouped[1][:], k_picked[:, :, PASS:N].rearrange("p j s -> p s j"))
 
         score = [sums_pool.tile([NQ, PASS], F32, name=f"score{h}") for h in range(PASSES)]
         capped = held.tile([NQ, N], F32, name="capped")
         minus_capped = held.tile([NQ, N], F32, name="minus_capped")
-        order = (1, 0)
         neg_max = [held.tile([NQ, 1], F32, name=f"neg_max{i}") for i in range(PASSES)]
         before = neg_sink
-        for i, h in enumerate(order):
+        for h in range(PASSES):
             cols = slice(h * PASS, (h + 1) * PASS)
+            nc.vector.tensor_copy(
+                k_grouped[:, cols, last],
+                k_pool[last][:].indirect(offsets[:, h * half_cols : (h + 1) * half_cols]),
+            )
             nc.vector.quantize_mx(
-                out=k_codes[h][:].bitcast(FP8X4), scales=k_scales[h][:], in_=k_grouped[h][:].rearrange("p s j -> p (s j)")
+                out=k_codes[h][:].bitcast(FP8X4), scales=k_scales[h][:], in_=k_grouped[:, cols, :].rearrange("p s j -> p (s j)")
             )
             nc.tensor.matmul_mx(
                 out=score[h][:],
@@ -124,18 +119,18 @@ def tile_attend_x_cap_sink_kernel(tc, qT, kT, vT, vs, sink, offs, out):
             )
             nc.scalar.activation(capped[:, cols], score[h][:], ACT.Tanh, scale=0.5)
             nc.vector.tensor_scalar(
-                minus_capped[:, cols], capped[:, cols], -2.0, before[:], ALU.mult, ALU.min, accum_out=neg_max[i][:]
+                minus_capped[:, cols], capped[:, cols], -2.0, before[:], ALU.mult, ALU.min, accum_out=neg_max[h][:]
             )
-            before = neg_max[i]
+            before = neg_max[h]
 
         p = held.tile([NQ, N], F32, name="p")
-        p_sum = [held.tile([NQ, 1], F32, name=f"p_sum{g}") for g in range(PASSES)]
+        terms = held.tile([NQ, PASSES + 1], F32, name="terms")
         w_codes = [held.tile([P, NQ], U32, align_bytes=64, name=f"w_codes{g}") for g in range(PASSES)]
         w_scales = [held.tile([P, NQ], U8, align_bytes=64, name=f"w_scales{g}") for g in range(PASSES)]
         for g in range(PASSES):
             cols = slice(g * PASS, (g + 1) * PASS)
             nc.scalar.activation(
-                p[:, cols], minus_capped[:, cols], ACT.Exp, bias=before[:], scale=-1.0, accum_out=p_sum[g][:]
+                p[:, cols], minus_capped[:, cols], ACT.Exp, bias=before[:], scale=-1.0, accum_out=terms[:, g : g + 1]
             )
             p_turned = turned_pool.tile([P, PACK, P], F32, tag="turned", name="p_turned")
             for t in range(PACK):
@@ -151,13 +146,10 @@ def tile_attend_x_cap_sink_kernel(tc, qT, kT, vT, vs, sink, offs, out):
                 out=w_codes[g][:].bitcast(FP8X4), scales=w_scales[g][:], in_=w_grouped[:].rearrange("p q j -> p (q j)")
             )
 
-        sink_term = held.tile([NQ, 1], F32, name="sink_term")
-        nc.scalar.activation(sink_term[:], sink_col[:], ACT.Exp, bias=before[:])
-        total0 = held.tile([NQ, 1], F32, name="total0")
+        nc.scalar.activation(terms[:, PASSES : PASSES + 1], sink_col[:], ACT.Exp, bias=before[:])
         total = held.tile([NQ, 1], F32, name="total")
         recip = held.tile([NQ, 1], F32, name="recip")
-        nc.vector.tensor_tensor(total0[:], p_sum[0][:], p_sum[1][:], ALU.add)
-        nc.vector.tensor_tensor(total[:], total0[:], sink_term[:], ALU.add)
+        nc.vector.reduce_sum(total[:], terms[:], mybir.AxisListType.X)
         nc.vector.reciprocal(recip[:], total[:])
 
         for b in range(EB):
@@ -191,5 +183,5 @@ def tile_attend_x_cap_sink_kernel(tc, qT, kT, vT, vs, sink, offs, out):
                     stop=(g == PASSES - 1),
                 )
             y_out = held.tile([NQ, P], F32, name=f"y_out{b}")
-            nc.vector.tensor_scalar(y_out[:], y[:], recip[:], None, ALU.mult)
+            nc.scalar.activation(y_out[:], y[:], ACT.Copy, scale=recip[:])
             nc.sync.dma_start(out[0, :, b * P : (b + 1) * P], y_out[:])

@@ -6,7 +6,7 @@ P = 128
 PACK = 4
 PASS = P * PACK
 PASSES = N // PASS
-EB = DV // P
+HALF_COLS = PASS // 16
 
 FLOPS = 2 * NQ * N * (D + DV)
 BYTES = 4 * (D * T + DV * T + D * NQ + T + NQ + NQ * DV) + 2 * P * (N // 16)
@@ -37,76 +37,92 @@ def tile_attend_x_cap_sink_kernel(tc, qT, kT, vT, vs, sink, offs, out):
         nc.scalar.activation(tiny_out[:], tiny[:], ACT.Exp)
 
         vs_pool = held.tile([P, T], F32, name="vs_pool")
-        nc.vector.memset(vs_pool[:], 0.0)
         sink_row = held.tile([P, P], F32, name="sink_row")
         nc.vector.memset(sink_row[:], 0.0)
+        nc.gpsimd.memset(vs_pool[:], 0.0)
         ident = held.tile([P, P], F32, name="ident")
         make_identity(nc, ident[:])
+        ident_bf = held.tile([P, P], BF16, name="ident_bf")
+        make_identity(nc, ident_bf[:])
 
         k_rows = kT.rearrange("(p j) t -> p j t", j=PACK)
         k_pool = [held.tile([P, T], F32, name=f"k_pool{j}") for j in range(PACK)]
-        v_pool = [held.tile([P, T], F32, name=f"v_pool{b}") for b in range(EB)]
+        v_pool = [held.tile([P, T], F32, name=f"v_pool{b}") for b in range(2)]
         q_raw = held.tile([P, PACK, NQ], F32, name="q_raw")
 
         nc.sync.dma_start(k_pool[0][:], k_rows[:, 0, :])
         nc.sync.dma_start(q_raw[:], qT[0].rearrange("(p j) w -> p j w", j=PACK))
         nc.sync.dma_start(sink_row[0:1, :], sink[0].rearrange("q o -> o q"))
         nc.sync.dma_start(vs_pool[0:1, :], vs[0:1, :])
-        for j in range(1, PACK):
-            nc.sync.dma_start(k_pool[j][:], k_rows[:, j, :])
-        for b in range(EB):
-            nc.sync.dma_start(v_pool[b][:], vT[b * P : (b + 1) * P, :])
+        nc.sync.dma_start(k_pool[1][:], k_rows[:, 1, :])
+        nc.sync.dma_start(k_pool[2][:], k_rows[:, 2, :])
+        nc.sync.dma_start(k_pool[3][:], k_rows[:, 3, :])
+        nc.sync.dma_start(v_pool[0][:], vT[0 * P : 1 * P, :])
+        nc.sync.dma_start(v_pool[1][:], vT[1 * P : 2 * P, :])
 
         q_grouped = held.tile([P, NQ, PACK], BF16, align_bytes=64, name="q_grouped")
         q_codes = held.tile([P, NQ], U32, align_bytes=64, name="q_codes")
         q_scales = held.tile([P, NQ], U8, align_bytes=64, name="q_scales")
-
-        k_grouped = held.tile([P, N, PACK], BF16, align_bytes=64, name="k_grouped")
-        nc.vector.tensor_copy(k_grouped[:, :, 0], k_pool[0][:].indirect(offsets[:]))
-        nc.scalar.copy(q_grouped[:], q_raw[:].rearrange("p j w -> p w j"))
-        nc.vector.quantize_mx(
-            out=q_codes[:].bitcast(FP8X4), scales=q_scales[:], in_=q_grouped[:].rearrange("p w j -> p (w j)")
-        )
-
-        sink_turned = turned_pool.tile([P, PACK, P], F32, tag="turned", name="sink_turned")
-        nc.tensor.transpose(sink_turned[:, 0, :], sink_row[:], ident[:])
         neg_sink = held.tile([P, 1], F32, name="neg_sink")
         sink_col = held.tile([P, 1], F32, name="sink_col")
-        nc.vector.tensor_scalar(neg_sink[:], sink_turned[:, 0, 0:1], -1.0, None, ALU.mult)
-        nc.vector.tensor_scalar(sink_col[:], neg_sink[:], -1.0, None, ALU.mult)
-
         vs_picked = held.tile([P, N], F32, name="vs_picked")
-        nc.vector.tensor_copy(vs_picked[:], vs_pool[:].indirect(offsets[:]))
         vs_cols = held.tile([P, PASSES, PACK], F32, name="vs_cols")
-        for g in range(PASSES):
-            vs_turned = turned_pool.tile([P, PACK, P], F32, tag="turned", name="vs_turned")
-            for t in range(PACK):
-                nc.tensor.transpose(
-                    vs_turned[:, t, :], vs_picked[:, g * PASS + t : (g + 1) * PASS : PACK], ident[:]
-                )
-            nc.scalar.copy(vs_cols[:, g, :], vs_turned[:, :, 0])
-
-        for j in range(1, PACK - 1):
-            nc.vector.tensor_copy(k_grouped[:, :, j], k_pool[j][:].indirect(offsets[:]))
-
-        half_cols = PASS // 16
-        last = PACK - 1
+        k_grouped = held.tile([P, N, PACK], BF16, align_bytes=64, name="k_grouped")
         k_codes = [held.tile([P, PASS], U32, align_bytes=64, name=f"k_codes{h}") for h in range(PASSES)]
         k_scales = [held.tile([P, PASS], U8, align_bytes=64, name=f"k_scales{h}") for h in range(PASSES)]
-
         score = [sums_pool.tile([NQ, PASS], F32, name=f"score{h}") for h in range(PASSES)]
         capped = held.tile([NQ, N], F32, name="capped")
         minus_capped = held.tile([NQ, N], F32, name="minus_capped")
-        neg_max = [held.tile([NQ, 1], F32, name=f"neg_max{i}") for i in range(PASSES)]
-        before = neg_sink
-        for h in range(PASSES):
-            cols = slice(h * PASS, (h + 1) * PASS)
-            nc.vector.tensor_copy(
-                k_grouped[:, cols, last],
-                k_pool[last][:].indirect(offsets[:, h * half_cols : (h + 1) * half_cols]),
-            )
+        neg_max = [held.tile([NQ, 1], F32, name=f"neg_max{h}") for h in range(PASSES)]
+        p = held.tile([NQ, PASSES, PACK, P], F32, name="p")
+        terms = held.tile([NQ, PASSES + 1], F32, name="terms")
+        w_grouped = [held.tile([P, NQ, PACK], BF16, align_bytes=64, name=f"w_grouped{g}") for g in range(PASSES)]
+        w_codes = [held.tile([P, NQ], U32, align_bytes=64, name=f"w_codes{g}") for g in range(PASSES)]
+        w_scales = [held.tile([P, NQ], U8, align_bytes=64, name=f"w_scales{g}") for g in range(PASSES)]
+        total = held.tile([NQ, 1], F32, name="total")
+        recip = held.tile([NQ, 1], F32, name="recip")
+        y = [sums_pool.tile([NQ, P], F32, name=f"y{b}") for b in range(2)]
+        v_codes = [[held.tile([P, P], U32, align_bytes=64, name=f"v_codes{b}{g}") for g in range(PASSES)] for b in range(2)]
+        v_scales = [[held.tile([P, P], U8, align_bytes=64, name=f"v_scales{b}{g}") for g in range(PASSES)] for b in range(2)]
+        v_picked = [held.tile([P, PASSES, PACK, P], BF16, name=f"v_picked{b}") for b in range(2)]
+
+        def queries():
+            nc.scalar.copy(q_grouped[:], q_raw[:].rearrange("p j w -> p w j"))
             nc.vector.quantize_mx(
-                out=k_codes[h][:].bitcast(FP8X4), scales=k_scales[h][:], in_=k_grouped[:, cols, :].rearrange("p s j -> p (s j)")
+                out=q_codes[:].bitcast(FP8X4), scales=q_scales[:], in_=q_grouped[:].rearrange("p w j -> p (w j)")
+            )
+
+        def sinks():
+            sink_turned = turned_pool.tile([P, PACK, P], F32, tag="turned", name="sink_turned")
+            nc.tensor.transpose(sink_turned[:, 0, :], sink_row[:], ident[:])
+            nc.vector.tensor_scalar(neg_sink[:], sink_turned[:, 0, 0:1], -1.0, None, ALU.mult)
+            nc.vector.tensor_scalar(sink_col[:], neg_sink[:], -1.0, None, ALU.mult)
+
+        def token_scales():
+            nc.vector.tensor_copy(vs_picked[:], vs_pool[:].indirect(offsets[:]))
+            for g in range(PASSES):
+                vs_turned = turned_pool.tile([P, PACK, P], F32, tag="turned", name="vs_turned")
+                for t in range(PACK):
+                    nc.tensor.transpose(
+                        vs_turned[:, t, :], vs_picked[:, g * PASS + t : (g + 1) * PASS : PACK], ident[:]
+                    )
+                nc.scalar.copy(vs_cols[:, g, :], vs_turned[:, :, 0])
+
+        def keys(j):
+            nc.vector.tensor_copy(k_grouped[:, :, j], k_pool[j][:].indirect(offsets[:]))
+
+        def keys_half(j, h):
+            nc.vector.tensor_copy(
+                k_grouped[:, h * PASS : (h + 1) * PASS, j],
+                k_pool[j][:].indirect(offsets[:, h * HALF_COLS : (h + 1) * HALF_COLS]),
+            )
+
+        def scores(h):
+            cols = slice(h * PASS, (h + 1) * PASS)
+            nc.vector.quantize_mx(
+                out=k_codes[h][:].bitcast(FP8X4),
+                scales=k_scales[h][:],
+                in_=k_grouped[:, cols, :].rearrange("p s j -> p (s j)"),
             )
             nc.tensor.matmul_mx(
                 out=score[h][:],
@@ -118,70 +134,112 @@ def tile_attend_x_cap_sink_kernel(tc, qT, kT, vT, vs, sink, offs, out):
                 stop=True,
             )
             nc.scalar.activation(capped[:, cols], score[h][:], ACT.Tanh, scale=0.5)
+
+        def maxima(h):
+            cols = slice(h * PASS, (h + 1) * PASS)
+            before = neg_sink if h == 0 else neg_max[h - 1]
             nc.vector.tensor_scalar(
                 minus_capped[:, cols], capped[:, cols], -2.0, before[:], ALU.mult, ALU.min, accum_out=neg_max[h][:]
             )
-            before = neg_max[h]
 
-        p = held.tile([NQ, N], F32, name="p")
-        terms = held.tile([NQ, PASSES + 1], F32, name="terms")
-        w_codes = [held.tile([P, NQ], U32, align_bytes=64, name=f"w_codes{g}") for g in range(PASSES)]
-        w_scales = [held.tile([P, NQ], U8, align_bytes=64, name=f"w_scales{g}") for g in range(PASSES)]
-        for g in range(PASSES):
+        def exps(g):
             cols = slice(g * PASS, (g + 1) * PASS)
             nc.scalar.activation(
-                p[:, cols], minus_capped[:, cols], ACT.Exp, bias=before[:], scale=-1.0, accum_out=terms[:, g : g + 1]
+                p[:, g].rearrange("q t s -> q s t"),
+                capped[:, cols].rearrange("q (s t) -> q s t", t=PACK),
+                ACT.Exp,
+                bias=neg_max[PASSES - 1][:],
+                scale=2.0,
+                accum_out=terms[:, g : g + 1],
             )
+
+        def weights(g):
             p_turned = turned_pool.tile([P, PACK, P], F32, tag="turned", name="p_turned")
             for t in range(PACK):
-                nc.tensor.transpose(p_turned[:, t, :], p[:, g * PASS + t : (g + 1) * PASS : PACK], ident[:])
-            w_grouped = held.tile([P, NQ, PACK], BF16, align_bytes=64, name=f"w_grouped{g}")
+                nc.tensor.transpose(p_turned[:, t, :], p[:, g, t, :], ident[:])
             nc.vector.tensor_tensor(
-                w_grouped[:],
+                w_grouped[g][:],
                 p_turned[:].rearrange("p j q -> p q j"),
                 vs_cols[:, g, :].unsqueeze(1).to_broadcast([P, NQ, PACK]),
                 ALU.mult,
             )
+
+        def weight_codes(g):
             nc.vector.quantize_mx(
-                out=w_codes[g][:].bitcast(FP8X4), scales=w_scales[g][:], in_=w_grouped[:].rearrange("p q j -> p (q j)")
+                out=w_codes[g][:].bitcast(FP8X4),
+                scales=w_scales[g][:],
+                in_=w_grouped[g][:].rearrange("p q j -> p (q j)"),
             )
 
-        nc.scalar.activation(terms[:, PASSES : PASSES + 1], sink_col[:], ACT.Exp, bias=before[:])
-        total = held.tile([NQ, 1], F32, name="total")
-        recip = held.tile([NQ, 1], F32, name="recip")
-        nc.vector.reduce_sum(total[:], terms[:], mybir.AxisListType.X)
-        nc.vector.reciprocal(recip[:], total[:])
+        def totals():
+            nc.scalar.activation(terms[:, PASSES : PASSES + 1], sink_col[:], ACT.Exp, bias=neg_max[PASSES - 1][:])
+            nc.vector.reduce_sum(total[:], terms[:], mybir.AxisListType.X)
+            nc.vector.reciprocal(recip[:], total[:])
 
-        for b in range(EB):
-            v_picked = held.tile([P, N], F32, name=f"v_picked{b}")
-            y = sums_pool.tile([NQ, P], F32, name=f"y{b}")
-            for g in range(PASSES):
-                nc.vector.tensor_copy(
-                    v_picked[:, g * PASS : (g + 1) * PASS],
-                    v_pool[b][:].indirect(offsets[:, g * half_cols : (g + 1) * half_cols]),
-                )
-            for g in range(PASSES):
-                v_turned = turned_pool.tile([P, PACK, P], F32, tag="turned", name="v_turned")
-                for t in range(PACK):
-                    nc.tensor.transpose(
-                        v_turned[:, t, :], v_picked[:, g * PASS + t : (g + 1) * PASS : PACK], ident[:]
-                    )
-                v_grouped = held.tile([P, P, PACK], BF16, align_bytes=64, name=f"v_grouped{b}{g}")
-                v_codes = held.tile([P, P], U32, align_bytes=64, name=f"v_codes{b}{g}")
-                v_scales = held.tile([P, P], U8, align_bytes=64, name=f"v_scales{b}{g}")
-                nc.scalar.copy(v_grouped[:], v_turned[:].rearrange("p j e -> p e j"))
-                nc.vector.quantize_mx(
-                    out=v_codes[:].bitcast(FP8X4), scales=v_scales[:], in_=v_grouped[:].rearrange("p e j -> p (e j)")
-                )
-                nc.tensor.matmul_mx(
-                    out=y[:],
-                    lhsT=w_codes[g][:].bitcast(FP8X4),
-                    lhsT_scale=w_scales[g][:],
-                    rhs=v_codes[:].bitcast(FP8X4),
-                    rhs_scale=v_scales[:],
-                    start=(g == 0),
-                    stop=(g == PASSES - 1),
-                )
+        def values(b, g):
+            nc.vector.tensor_copy(
+                v_picked[b][:, g].rearrange("p t s -> p s t"),
+                v_pool[b][:].indirect(offsets[:, g * HALF_COLS : (g + 1) * HALF_COLS]),
+            )
+
+        def value_codes(b, g):
+            v_turned = turned_pool.tile([P, PACK, P], BF16, tag="turned", name="v_turned")
+            for t in range(PACK):
+                nc.tensor.transpose(v_turned[:, t, :], v_picked[b][:, g, t, :], ident_bf[:])
+            v_grouped = held.tile([P, P, PACK], BF16, align_bytes=64, name=f"v_grouped{b}{g}")
+            nc.scalar.copy(v_grouped[:], v_turned[:].rearrange("p j e -> p e j"))
+            nc.vector.quantize_mx(
+                out=v_codes[b][g][:].bitcast(FP8X4),
+                scales=v_scales[b][g][:],
+                in_=v_grouped[:].rearrange("p e j -> p (e j)"),
+            )
+
+        def products(b, g):
+            nc.tensor.matmul_mx(
+                out=y[b][:],
+                lhsT=w_codes[g][:].bitcast(FP8X4),
+                lhsT_scale=w_scales[g][:],
+                rhs=v_codes[b][g][:].bitcast(FP8X4),
+                rhs_scale=v_scales[b][g][:],
+                start=(g == 0),
+                stop=(g == PASSES - 1),
+            )
+
+        def result(b):
             y_out = held.tile([NQ, P], F32, name=f"y_out{b}")
-            nc.scalar.activation(y_out[:], y[:], ACT.Copy, scale=recip[:])
+            nc.scalar.activation(y_out[:], y[b][:], ACT.Copy, scale=recip[:])
             nc.sync.dma_start(out[0, :, b * P : (b + 1) * P], y_out[:])
+
+        keys(0)
+        queries()
+        sinks()
+        keys(1)
+        token_scales()
+        keys(2)
+        keys_half(3, 0)
+        scores(0)
+        keys_half(3, 1)
+        scores(1)
+        maxima(0)
+        maxima(1)
+        values(0, 0)
+        exps(0)
+        exps(1)
+        weights(0)
+        values(0, 1)
+        weights(1)
+        weight_codes(0)
+        weight_codes(1)
+        totals()
+        value_codes(0, 0)
+        value_codes(0, 1)
+        values(1, 0)
+        values(1, 1)
+        products(0, 0)
+        products(0, 1)
+        result(0)
+        value_codes(1, 0)
+        value_codes(1, 1)
+        products(1, 0)
+        products(1, 1)
+        result(1)

@@ -6,7 +6,7 @@ P = 128
 PACK = 4
 PASS = P * PACK
 PASSES = N // PASS
-HALF_COLS = PASS // 16
+LIST_ROWS = 16
 
 FLOPS = 2 * NQ * N * (D + DV)
 BYTES = 4 * (D * T + DV * T + D * NQ + T + NQ + NQ * DV) + 2 * P * (N // 16)
@@ -19,6 +19,8 @@ U8 = mybir.dt.uint8
 FP8X4 = mybir.dt.float8_e4m3fn_x4
 ACT = mybir.ActivationFunctionType
 ALU = mybir.AluOpType
+W_SLOT = ("w_slot", "v_slot1")
+PIECES = ((0, 512), (512, 1024))
 
 
 def tile_attend_x_cap_sink_kernel(tc, qT, kT, vT, vs, sink, offs, out):
@@ -28,8 +30,11 @@ def tile_attend_x_cap_sink_kernel(tc, qT, kT, vT, vs, sink, offs, out):
         tc.psum_pool(name="turned", bufs=4) as turned_pool,
         tc.psum_pool(name="sums", bufs=1) as sums_pool,
     ):
-        offsets = held.tile([P, N // 16], U16, name="offsets")
+        offsets = held.tile([P, N // LIST_ROWS], U16, name="offsets")
         nc.sync.dma_start(offsets[:], offs)
+
+        def listed(window, start, stop):
+            return window[:].indirect(offsets[:, start // LIST_ROWS : stop // LIST_ROWS])
 
         tiny = held.tile([P, 1], F32, name="tiny")
         nc.vector.memset(tiny[:], 0.0)
@@ -39,7 +44,7 @@ def tile_attend_x_cap_sink_kernel(tc, qT, kT, vT, vs, sink, offs, out):
         vs_pool = held.tile([P, T], F32, name="vs_pool")
         sink_row = held.tile([P, P], F32, name="sink_row")
         nc.vector.memset(sink_row[:], 0.0)
-        nc.gpsimd.memset(vs_pool[:], 0.0)
+        nc.vector.memset(vs_pool[:], 0.0)
         ident = held.tile([P, P], F32, name="ident")
         make_identity(nc, ident[:])
         ident_bf = held.tile([P, P], BF16, name="ident_bf")
@@ -47,16 +52,16 @@ def tile_attend_x_cap_sink_kernel(tc, qT, kT, vT, vs, sink, offs, out):
 
         k_rows = kT.rearrange("(p j) t -> p j t", j=PACK)
         k_pool = [held.tile([P, T], F32, name=f"k_pool{j}") for j in range(PACK)]
-        v_pool = [held.tile([P, T], F32, name=f"v_pool{b}") for b in range(2)]
+        v_pool = [held.tile([P, T], F32, align_bytes=64, tag=f"v_slot{b}", name=f"v_pool{b}") for b in range(2)]
         q_raw = held.tile([P, PACK, NQ], F32, name="q_raw")
 
         nc.sync.dma_start(k_pool[0][:], k_rows[:, 0, :])
-        nc.sync.dma_start(q_raw[:], qT[0].rearrange("(p j) w -> p j w", j=PACK))
+        nc.sync.dma_start(k_pool[1][:], k_rows[:, 1, :])
         nc.sync.dma_start(sink_row[0:1, :], sink[0].rearrange("q o -> o q"))
         nc.sync.dma_start(vs_pool[0:1, :], vs[0:1, :])
-        nc.sync.dma_start(k_pool[1][:], k_rows[:, 1, :])
         nc.sync.dma_start(k_pool[2][:], k_rows[:, 2, :])
         nc.sync.dma_start(k_pool[3][:], k_rows[:, 3, :])
+        nc.sync.dma_start(q_raw[:], qT[0].rearrange("(p j) w -> p j w", j=PACK))
         nc.sync.dma_start(v_pool[0][:], vT[0 * P : 1 * P, :])
         nc.sync.dma_start(v_pool[1][:], vT[1 * P : 2 * P, :])
 
@@ -68,23 +73,23 @@ def tile_attend_x_cap_sink_kernel(tc, qT, kT, vT, vs, sink, offs, out):
         vs_picked = held.tile([P, N], F32, name="vs_picked")
         vs_cols = held.tile([P, PASSES, PACK], F32, name="vs_cols")
         k_grouped = held.tile([P, N, PACK], BF16, align_bytes=64, name="k_grouped")
-        k_codes = [held.tile([P, PASS], U32, align_bytes=64, name=f"k_codes{h}") for h in range(PASSES)]
-        k_scales = [held.tile([P, PASS], U8, align_bytes=64, name=f"k_scales{h}") for h in range(PASSES)]
-        score = [sums_pool.tile([NQ, PASS], F32, name=f"score{h}") for h in range(PASSES)]
+        k_codes = [held.tile([P, b - a], U32, align_bytes=64, name=f"k_codes{i}") for i, (a, b) in enumerate(PIECES)]
+        k_scales = [held.tile([P, b - a], U8, align_bytes=64, name=f"k_scales{i}") for i, (a, b) in enumerate(PIECES)]
+        score = [sums_pool.tile([NQ, b - a], F32, name=f"score{i}") for i, (a, b) in enumerate(PIECES)]
         capped = held.tile([NQ, N], F32, name="capped")
         minus_capped = held.tile([NQ, N], F32, name="minus_capped")
-        neg_max = [held.tile([NQ, 1], F32, name=f"neg_max{h}") for h in range(PASSES)]
+        neg_max = [held.tile([NQ, 1], F32, name=f"neg_max{i}") for i in range(len(PIECES))]
         p = held.tile([NQ, PASSES, PACK, P], F32, name="p")
         terms = held.tile([NQ, PASSES + 1], F32, name="terms")
-        w_grouped = [held.tile([P, NQ, PACK], BF16, align_bytes=64, name=f"w_grouped{g}") for g in range(PASSES)]
         w_codes = [held.tile([P, NQ], U32, align_bytes=64, name=f"w_codes{g}") for g in range(PASSES)]
         w_scales = [held.tile([P, NQ], U8, align_bytes=64, name=f"w_scales{g}") for g in range(PASSES)]
         total = held.tile([NQ, 1], F32, name="total")
         recip = held.tile([NQ, 1], F32, name="recip")
-        y = [sums_pool.tile([NQ, P], F32, name=f"y{b}") for b in range(2)]
-        v_codes = [[held.tile([P, P], U32, align_bytes=64, name=f"v_codes{b}{g}") for g in range(PASSES)] for b in range(2)]
-        v_scales = [[held.tile([P, P], U8, align_bytes=64, name=f"v_scales{b}{g}") for g in range(PASSES)] for b in range(2)]
-        v_picked = [held.tile([P, PASSES, PACK, P], BF16, name=f"v_picked{b}") for b in range(2)]
+        v0_picked = held.tile([P, N], F32, name="v0_picked")
+        v1_picked = held.tile([P, PASSES, PACK, P], BF16, name="v1_picked")
+        v_grouped = [held.tile([P, 2, P, PACK], BF16, align_bytes=64, name=f"v_grouped{g}") for g in range(PASSES)]
+        v_codes = [held.tile([P, DV], U32, align_bytes=64, name=f"v_codes{g}") for g in range(PASSES)]
+        v_scales = [held.tile([P, DV], U8, align_bytes=64, name=f"v_scales{g}") for g in range(PASSES)]
 
         def queries():
             nc.scalar.copy(q_grouped[:], q_raw[:].rearrange("p j w -> p w j"))
@@ -99,7 +104,7 @@ def tile_attend_x_cap_sink_kernel(tc, qT, kT, vT, vs, sink, offs, out):
             nc.vector.tensor_scalar(sink_col[:], neg_sink[:], -1.0, None, ALU.mult)
 
         def token_scales():
-            nc.vector.tensor_copy(vs_picked[:], vs_pool[:].indirect(offsets[:]))
+            nc.vector.tensor_copy(vs_picked[:], listed(vs_pool, 0, N))
             for g in range(PASSES):
                 vs_turned = turned_pool.tile([P, PACK, P], F32, tag="turned", name="vs_turned")
                 for t in range(PACK):
@@ -108,47 +113,46 @@ def tile_attend_x_cap_sink_kernel(tc, qT, kT, vT, vs, sink, offs, out):
                     )
                 nc.scalar.copy(vs_cols[:, g, :], vs_turned[:, :, 0])
 
-        def keys(j):
-            nc.vector.tensor_copy(k_grouped[:, :, j], k_pool[j][:].indirect(offsets[:]))
+        def keys(j, start=0, stop=N):
+            nc.vector.tensor_copy(k_grouped[:, start:stop, j], listed(k_pool[j], start, stop))
 
-        def keys_half(j, h):
-            nc.vector.tensor_copy(
-                k_grouped[:, h * PASS : (h + 1) * PASS, j],
-                k_pool[j][:].indirect(offsets[:, h * HALF_COLS : (h + 1) * HALF_COLS]),
-            )
-
-        def scores(h):
-            cols = slice(h * PASS, (h + 1) * PASS)
+        def scores(i):
+            start, stop = PIECES[i]
             nc.vector.quantize_mx(
-                out=k_codes[h][:].bitcast(FP8X4),
-                scales=k_scales[h][:],
-                in_=k_grouped[:, cols, :].rearrange("p s j -> p (s j)"),
+                out=k_codes[i][:].bitcast(FP8X4),
+                scales=k_scales[i][:],
+                in_=k_grouped[:, start:stop, :].rearrange("p s j -> p (s j)"),
             )
             nc.tensor.matmul_mx(
-                out=score[h][:],
+                out=score[i][:],
                 lhsT=q_codes[:].bitcast(FP8X4),
                 lhsT_scale=q_scales[:],
-                rhs=k_codes[h][:].bitcast(FP8X4),
-                rhs_scale=k_scales[h][:],
+                rhs=k_codes[i][:].bitcast(FP8X4),
+                rhs_scale=k_scales[i][:],
                 start=True,
                 stop=True,
             )
-            nc.scalar.activation(capped[:, cols], score[h][:], ACT.Tanh, scale=0.5)
+            nc.scalar.activation(capped[:, start:stop], score[i][:], ACT.Tanh, scale=0.5)
 
-        def maxima(h):
-            cols = slice(h * PASS, (h + 1) * PASS)
-            before = neg_sink if h == 0 else neg_max[h - 1]
+        def maxima(i):
+            start, stop = PIECES[i]
+            before = neg_sink if i == 0 else neg_max[i - 1]
             nc.vector.tensor_scalar(
-                minus_capped[:, cols], capped[:, cols], -2.0, before[:], ALU.mult, ALU.min, accum_out=neg_max[h][:]
+                minus_capped[:, start:stop],
+                capped[:, start:stop],
+                -2.0,
+                before[:],
+                ALU.mult,
+                ALU.min,
+                accum_out=neg_max[i][:],
             )
 
         def exps(g):
-            cols = slice(g * PASS, (g + 1) * PASS)
             nc.scalar.activation(
                 p[:, g].rearrange("q t s -> q s t"),
-                capped[:, cols].rearrange("q (s t) -> q s t", t=PACK),
+                capped[:, g * PASS : (g + 1) * PASS].rearrange("q (s t) -> q s t", t=PACK),
                 ACT.Exp,
-                bias=neg_max[PASSES - 1][:],
+                bias=neg_max[-1][:],
                 scale=2.0,
                 accum_out=terms[:, g : g + 1],
             )
@@ -157,89 +161,93 @@ def tile_attend_x_cap_sink_kernel(tc, qT, kT, vT, vs, sink, offs, out):
             p_turned = turned_pool.tile([P, PACK, P], F32, tag="turned", name="p_turned")
             for t in range(PACK):
                 nc.tensor.transpose(p_turned[:, t, :], p[:, g, t, :], ident[:])
+            w_grouped = held.tile([P, NQ, PACK], BF16, align_bytes=64, tag=W_SLOT[g], name=f"w_grouped{g}")
             nc.vector.tensor_tensor(
-                w_grouped[g][:],
+                w_grouped[:],
                 p_turned[:].rearrange("p j q -> p q j"),
                 vs_cols[:, g, :].unsqueeze(1).to_broadcast([P, NQ, PACK]),
                 ALU.mult,
             )
+            return w_grouped
 
-        def weight_codes(g):
+        def weight_codes(g, w_grouped):
             nc.vector.quantize_mx(
                 out=w_codes[g][:].bitcast(FP8X4),
                 scales=w_scales[g][:],
-                in_=w_grouped[g][:].rearrange("p q j -> p (q j)"),
+                in_=w_grouped[:].rearrange("p q j -> p (q j)"),
             )
 
         def totals():
-            nc.scalar.activation(terms[:, PASSES : PASSES + 1], sink_col[:], ACT.Exp, bias=neg_max[PASSES - 1][:])
+            nc.scalar.activation(terms[:, PASSES : PASSES + 1], sink_col[:], ACT.Exp, bias=neg_max[-1][:])
             nc.vector.reduce_sum(total[:], terms[:], mybir.AxisListType.X)
             nc.vector.reciprocal(recip[:], total[:])
 
         def values(b, g):
-            nc.vector.tensor_copy(
-                v_picked[b][:, g].rearrange("p t s -> p s t"),
-                v_pool[b][:].indirect(offsets[:, g * HALF_COLS : (g + 1) * HALF_COLS]),
-            )
+            picked = v1_picked[:, g].rearrange("p t s -> p s t") if b else v0_picked[:, g * PASS : (g + 1) * PASS]
+            nc.vector.tensor_copy(picked, listed(v_pool[b], g * PASS, (g + 1) * PASS))
 
-        def value_codes(b, g):
-            v_turned = turned_pool.tile([P, PACK, P], BF16, tag="turned", name="v_turned")
+        def turn_values(b, g):
+            v_turned = turned_pool.tile([P, PACK, P], BF16 if b else F32, tag="turned", name="v_turned")
             for t in range(PACK):
-                nc.tensor.transpose(v_turned[:, t, :], v_picked[b][:, g, t, :], ident_bf[:])
-            v_grouped = held.tile([P, P, PACK], BF16, align_bytes=64, name=f"v_grouped{b}{g}")
-            nc.scalar.copy(v_grouped[:], v_turned[:].rearrange("p j e -> p e j"))
+                if b:
+                    nc.tensor.transpose(v_turned[:, t, :], v1_picked[:, g, t, :], ident_bf[:])
+                else:
+                    nc.tensor.transpose(v_turned[:, t, :], v0_picked[:, g * PASS + t : (g + 1) * PASS : PACK], ident[:])
+            nc.scalar.copy(v_grouped[g][:, b], v_turned[:].rearrange("p j e -> p e j"))
+
+        def value_codes(g):
             nc.vector.quantize_mx(
-                out=v_codes[b][g][:].bitcast(FP8X4),
-                scales=v_scales[b][g][:],
-                in_=v_grouped[:].rearrange("p e j -> p (e j)"),
+                out=v_codes[g][:].bitcast(FP8X4),
+                scales=v_scales[g][:],
+                in_=v_grouped[g][:].rearrange("p b e j -> p (b e j)"),
             )
 
-        def products(b, g):
+        def products(y, g, first, last):
             nc.tensor.matmul_mx(
-                out=y[b][:],
+                out=y[:],
                 lhsT=w_codes[g][:].bitcast(FP8X4),
                 lhsT_scale=w_scales[g][:],
-                rhs=v_codes[b][g][:].bitcast(FP8X4),
-                rhs_scale=v_scales[b][g][:],
+                rhs=v_codes[g][:, first:last].bitcast(FP8X4),
+                rhs_scale=v_scales[g][:, first:last],
                 start=(g == 0),
                 stop=(g == PASSES - 1),
             )
 
-        def result(b):
-            y_out = held.tile([NQ, P], F32, name=f"y_out{b}")
-            nc.scalar.activation(y_out[:], y[b][:], ACT.Copy, scale=recip[:])
-            nc.sync.dma_start(out[0, :, b * P : (b + 1) * P], y_out[:])
+        def result(y, first, last):
+            y_out = held.tile([NQ, last - first], F32, name=f"y_out{first}")
+            nc.scalar.activation(y_out[:], y[:], ACT.Copy, scale=recip[:])
+            nc.sync.dma_start(out[0, :, first:last], y_out[:])
 
         keys(0)
         queries()
-        sinks()
         keys(1)
+        sinks()
         token_scales()
         keys(2)
-        keys_half(3, 0)
+        keys(3, 0, 512)
         scores(0)
-        keys_half(3, 1)
+        keys(3, 512, 1024)
         scores(1)
         maxima(0)
         maxima(1)
-        values(0, 0)
         exps(0)
         exps(1)
-        weights(0)
+        values(0, 0)
         values(0, 1)
-        weights(1)
-        weight_codes(0)
-        weight_codes(1)
-        totals()
-        value_codes(0, 0)
-        value_codes(0, 1)
+        w0 = weights(0)
         values(1, 0)
         values(1, 1)
-        products(0, 0)
-        products(0, 1)
-        result(0)
-        value_codes(1, 0)
-        value_codes(1, 1)
-        products(1, 0)
-        products(1, 1)
-        result(1)
+        w1 = weights(1)
+        turn_values(0, 0)
+        turn_values(0, 1)
+        turn_values(1, 0)
+        turn_values(1, 1)
+        weight_codes(0, w0)
+        weight_codes(1, w1)
+        totals()
+        value_codes(0)
+        value_codes(1)
+        y = sums_pool.tile([NQ, DV], F32, name="y")
+        products(y, 0, 0, DV)
+        products(y, 1, 0, DV)
+        result(y, 0, DV)

@@ -19,7 +19,6 @@ U8 = mybir.dt.uint8
 FP8X4 = mybir.dt.float8_e4m3fn_x4
 ACT = mybir.ActivationFunctionType
 ALU = mybir.AluOpType
-W_SLOT = ("w_slot", "v_slot1")
 PIECES = ((0, 512), (512, 1024))
 
 
@@ -27,6 +26,8 @@ def tile_attend_x_cap_sink_kernel(tc, qT, kT, vT, vs, sink, offs, out):
     nc = tc.nc
     with (
         tc.tile_pool(name="held", bufs=1) as held,
+        tc.tile_pool(name="shared0", bufs=1) as shared0,
+        tc.tile_pool(name="shared1", bufs=1) as shared1,
         tc.psum_pool(name="turned", bufs=4) as turned_pool,
         tc.psum_pool(name="sums", bufs=1) as sums_pool,
     ):
@@ -52,7 +53,10 @@ def tile_attend_x_cap_sink_kernel(tc, qT, kT, vT, vs, sink, offs, out):
 
         k_rows = kT.rearrange("(p j) t -> p j t", j=PACK)
         k_pool = [held.tile([P, T], F32, name=f"k_pool{j}") for j in range(PACK)]
-        v_pool = [held.tile([P, T], F32, align_bytes=64, tag=f"v_slot{b}", name=f"v_pool{b}") for b in range(2)]
+        v_pool = [
+            shared0.tile([P, T], F32, align_bytes=64, offset=0, name="v_pool0"),
+            shared1.tile([P, T], F32, align_bytes=64, offset=0, name="v_pool1"),
+        ]
         q_raw = held.tile([P, PACK, NQ], F32, name="q_raw")
 
         nc.sync.dma_start(k_pool[0][:], k_rows[:, 0, :])
@@ -77,19 +81,16 @@ def tile_attend_x_cap_sink_kernel(tc, qT, kT, vT, vs, sink, offs, out):
         k_scales = [held.tile([P, b - a], U8, align_bytes=64, name=f"k_scales{i}") for i, (a, b) in enumerate(PIECES)]
         score = [sums_pool.tile([NQ, b - a], F32, name=f"score{i}") for i, (a, b) in enumerate(PIECES)]
         capped = held.tile([NQ, N], F32, name="capped")
-        minus_capped = held.tile([NQ, N], F32, name="minus_capped")
         neg_max = [held.tile([NQ, 1], F32, name=f"neg_max{i}") for i in range(len(PIECES))]
         p = held.tile([NQ, PASSES, PACK, P], F32, name="p")
         terms = held.tile([NQ, PASSES + 1], F32, name="terms")
         w_codes = [held.tile([P, NQ], U32, align_bytes=64, name=f"w_codes{g}") for g in range(PASSES)]
         w_scales = [held.tile([P, NQ], U8, align_bytes=64, name=f"w_scales{g}") for g in range(PASSES)]
-        total = held.tile([NQ, 1], F32, name="total")
         recip = held.tile([NQ, 1], F32, name="recip")
         v0_picked = held.tile([P, N], F32, name="v0_picked")
         v1_picked = held.tile([P, PASSES, PACK, P], BF16, name="v1_picked")
-        v_grouped = [held.tile([P, 2, P, PACK], BF16, align_bytes=64, name=f"v_grouped{g}") for g in range(PASSES)]
-        v_codes = [held.tile([P, DV], U32, align_bytes=64, name=f"v_codes{g}") for g in range(PASSES)]
-        v_scales = [held.tile([P, DV], U8, align_bytes=64, name=f"v_scales{g}") for g in range(PASSES)]
+        v_grouped = [held.tile([P, PASSES, P, PACK], BF16, align_bytes=64, name=f"v_grouped{b}") for b in range(2)]
+        v_scales = [held.tile([P, PASSES * P], U8, align_bytes=64, name=f"v_scales{b}") for b in range(2)]
 
         def queries():
             nc.scalar.copy(q_grouped[:], q_raw[:].rearrange("p j w -> p w j"))
@@ -161,7 +162,7 @@ def tile_attend_x_cap_sink_kernel(tc, qT, kT, vT, vs, sink, offs, out):
             p_turned = turned_pool.tile([P, PACK, P], F32, tag="turned", name="p_turned")
             for t in range(PACK):
                 nc.tensor.transpose(p_turned[:, t, :], p[:, g, t, :], ident[:])
-            w_grouped = held.tile([P, NQ, PACK], BF16, align_bytes=64, tag=W_SLOT[g], name=f"w_grouped{g}")
+            w_grouped = shared1.tile([P, NQ, PACK], BF16, align_bytes=64, offset=g * NQ * PACK * 2, name=f"w_grouped{g}")
             nc.vector.tensor_tensor(
                 w_grouped[:],
                 p_turned[:].rearrange("p j q -> p q j"),
@@ -193,25 +194,28 @@ def tile_attend_x_cap_sink_kernel(tc, qT, kT, vT, vs, sink, offs, out):
                     nc.tensor.transpose(v_turned[:, t, :], v1_picked[:, g, t, :], ident_bf[:])
                 else:
                     nc.tensor.transpose(v_turned[:, t, :], v0_picked[:, g * PASS + t : (g + 1) * PASS : PACK], ident[:])
-            nc.scalar.copy(v_grouped[g][:, b], v_turned[:].rearrange("p j e -> p e j"))
+            nc.scalar.copy(v_grouped[b][:, g], v_turned[:].rearrange("p j e -> p e j"))
 
-        def value_codes(g):
+        def value_codes(b, v_codes, first, last):
             nc.vector.quantize_mx(
-                out=v_codes[g][:].bitcast(FP8X4),
-                scales=v_scales[g][:],
-                in_=v_grouped[g][:].rearrange("p b e j -> p (b e j)"),
+                out=v_codes[:, first * P : last * P].bitcast(FP8X4),
+                scales=v_scales[b][:, first * P : last * P],
+                in_=v_grouped[b][:, first:last].rearrange("p g e j -> p (g e j)"),
             )
 
-        def products(y, g, first, last):
-            nc.tensor.matmul_mx(
-                out=y[:],
-                lhsT=w_codes[g][:].bitcast(FP8X4),
-                lhsT_scale=w_scales[g][:],
-                rhs=v_codes[g][:, first:last].bitcast(FP8X4),
-                rhs_scale=v_scales[g][:, first:last],
-                start=(g == 0),
-                stop=(g == PASSES - 1),
-            )
+        def products(b, v_codes):
+            y = sums_pool.tile([NQ, P], F32, name=f"y{b}")
+            for g in range(PASSES):
+                nc.tensor.matmul_mx(
+                    out=y[:],
+                    lhsT=w_codes[g][:].bitcast(FP8X4),
+                    lhsT_scale=w_scales[g][:],
+                    rhs=v_codes[:, g * P : (g + 1) * P].bitcast(FP8X4),
+                    rhs_scale=v_scales[b][:, g * P : (g + 1) * P],
+                    start=(g == 0),
+                    stop=(g == PASSES - 1),
+                )
+            result(y, b * P, (b + 1) * P)
 
         def result(y, first, last):
             y_out = held.tile([NQ, last - first], F32, name=f"y_out{first}")
@@ -228,15 +232,16 @@ def tile_attend_x_cap_sink_kernel(tc, qT, kT, vT, vs, sink, offs, out):
         scores(0)
         keys(3, 512, 1024)
         scores(1)
+        values(0, 0)
+        values(0, 1)
+        minus_capped = shared0.tile([NQ, N], F32, align_bytes=64, offset=0, name="minus_capped")
         maxima(0)
         maxima(1)
         exps(0)
         exps(1)
-        values(0, 0)
-        values(0, 1)
-        w0 = weights(0)
         values(1, 0)
         values(1, 1)
+        w0 = weights(0)
         w1 = weights(1)
         turn_values(0, 0)
         turn_values(0, 1)
@@ -244,10 +249,12 @@ def tile_attend_x_cap_sink_kernel(tc, qT, kT, vT, vs, sink, offs, out):
         turn_values(1, 1)
         weight_codes(0, w0)
         weight_codes(1, w1)
+        total = shared1.tile([NQ, 1], F32, align_bytes=64, offset=2 * NQ * PACK * 2, name="total")
         totals()
-        value_codes(0)
-        value_codes(1)
-        y = sums_pool.tile([NQ, DV], F32, name="y")
-        products(y, 0, 0, DV)
-        products(y, 1, 0, DV)
-        result(y, 0, DV)
+        v_codes0 = held.tile([P, PASSES * P], U32, align_bytes=64, name="v_codes0")
+        value_codes(0, v_codes0, 0, 2)
+        v_codes1 = held.tile([P, PASSES * P], U32, align_bytes=64, name="v_codes1")
+        value_codes(1, v_codes1, 0, 1)
+        value_codes(1, v_codes1, 1, 2)
+        products(0, v_codes0)
+        products(1, v_codes1)

import concourse.mybir as mybir
from concourse.masks import make_identity

NQ, D, DV, T, N = 128, 512, 256, 4096, 1024
P = 128
PACK = 4
PASS = P * PACK
PASSES = N // PASS
LIST_ROWS = 16

FLOPS = 2 * NQ * N * (D + DV)
BYTES = 4 * (D * T + DV * T + D * NQ + T + NQ + NQ * DV) + 2 * P * (N // 16)

F32 = mybir.dt.float32
BF16 = mybir.dt.bfloat16
U32 = mybir.dt.uint32
U16 = mybir.dt.uint16
U8 = mybir.dt.uint8
FP8X4 = mybir.dt.float8_e4m3fn_x4
ACT = mybir.ActivationFunctionType
ALU = mybir.AluOpType
PIECES = ((0, 512), (512, 1024))


def tile_attend_x_cap_sink_kernel(tc, qT, kT, vT, vs, sink, offs, out):
    nc = tc.nc
    with (
        tc.tile_pool(name="held", bufs=1) as held,
        tc.tile_pool(name="shared0", bufs=1) as shared0,
        tc.tile_pool(name="shared1", bufs=1) as shared1,
        tc.psum_pool(name="turned", bufs=4) as turned_pool,
        tc.psum_pool(name="sums", bufs=1) as sums_pool,
    ):
        offsets = held.tile([P, N // LIST_ROWS], U16, name="offsets")
        nc.sync.dma_start(offsets[:], offs)

        def listed(window, start, stop):
            return window[:].indirect(offsets[:, start // LIST_ROWS : stop // LIST_ROWS])

        tiny = held.tile([P, 1], F32, name="tiny")
        nc.vector.memset(tiny[:], 0.0)
        tiny_out = held.tile([P, 1], F32, name="tiny_out")
        nc.scalar.activation(tiny_out[:], tiny[:], ACT.Exp)

        vs_pool = held.tile([P, T], F32, name="vs_pool")
        sink_row = held.tile([P, P], F32, name="sink_row")
        nc.vector.memset(sink_row[:], 0.0)
        nc.vector.memset(vs_pool[:], 0.0)
        ident = held.tile([P, P], F32, name="ident")
        make_identity(nc, ident[:])
        ident_bf = held.tile([P, P], BF16, name="ident_bf")
        make_identity(nc, ident_bf[:])

        k_rows = kT.rearrange("(p j) t -> p j t", j=PACK)
        k_pool = [held.tile([P, T], F32, name=f"k_pool{j}") for j in range(PACK)]
        v_pool = [
            shared0.tile([P, T], F32, align_bytes=64, offset=0, name="v_pool0"),
            shared1.tile([P, T], F32, align_bytes=64, offset=0, name="v_pool1"),
        ]
        q_raw = held.tile([P, PACK, NQ], F32, name="q_raw")

        nc.sync.dma_start(k_pool[0][:], k_rows[:, 0, :])
        nc.sync.dma_start(k_pool[1][:], k_rows[:, 1, :])
        nc.sync.dma_start(sink_row[0:1, :], sink[0].rearrange("q o -> o q"))
        nc.sync.dma_start(vs_pool[0:1, :], vs[0:1, :])
        nc.sync.dma_start(k_pool[2][:], k_rows[:, 2, :])
        nc.sync.dma_start(k_pool[3][:], k_rows[:, 3, :])
        nc.sync.dma_start(q_raw[:], qT[0].rearrange("(p j) w -> p j w", j=PACK))
        nc.sync.dma_start(v_pool[0][:], vT[0 * P : 1 * P, :])
        nc.sync.dma_start(v_pool[1][:], vT[1 * P : 2 * P, :])

        q_grouped = held.tile([P, NQ, PACK], BF16, align_bytes=64, name="q_grouped")
        q_codes = held.tile([P, NQ], U32, align_bytes=64, name="q_codes")
        q_scales = held.tile([P, NQ], U8, align_bytes=64, name="q_scales")
        neg_sink = held.tile([P, 1], F32, name="neg_sink")
        sink_col = held.tile([P, 1], F32, name="sink_col")
        vs_picked = held.tile([P, N], F32, name="vs_picked")
        vs_cols = held.tile([P, PASSES, PACK], F32, name="vs_cols")
        k_grouped = held.tile([P, N, PACK], BF16, align_bytes=64, name="k_grouped")
        k_codes = [held.tile([P, b - a], U32, align_bytes=64, name=f"k_codes{i}") for i, (a, b) in enumerate(PIECES)]
        k_scales = [held.tile([P, b - a], U8, align_bytes=64, name=f"k_scales{i}") for i, (a, b) in enumerate(PIECES)]
        score = [sums_pool.tile([NQ, b - a], F32, name=f"score{i}") for i, (a, b) in enumerate(PIECES)]
        capped = held.tile([NQ, N], F32, name="capped")
        neg_max = [held.tile([NQ, 1], F32, name=f"neg_max{i}") for i in range(len(PIECES))]
        p = held.tile([NQ, PASSES, PACK, P], F32, name="p")
        terms = held.tile([NQ, PASSES + 1], F32, name="terms")
        w_codes = [held.tile([P, NQ], U32, align_bytes=64, name=f"w_codes{g}") for g in range(PASSES)]
        w_scales = [held.tile([P, NQ], U8, align_bytes=64, name=f"w_scales{g}") for g in range(PASSES)]
        recip = held.tile([NQ, 1], F32, name="recip")
        v0_picked = held.tile([P, N], F32, name="v0_picked")
        v1_picked = held.tile([P, PASSES, PACK, P], BF16, name="v1_picked")
        v_grouped = [held.tile([P, PASSES, P, PACK], BF16, align_bytes=64, name=f"v_grouped{b}") for b in range(2)]
        v_scales = [held.tile([P, PASSES * P], U8, align_bytes=64, name=f"v_scales{b}") for b in range(2)]

        def queries():
            nc.scalar.copy(q_grouped[:], q_raw[:].rearrange("p j w -> p w j"))
            nc.vector.quantize_mx(
                out=q_codes[:].bitcast(FP8X4), scales=q_scales[:], in_=q_grouped[:].rearrange("p w j -> p (w j)")
            )

        def sinks():
            sink_turned = turned_pool.tile([P, PACK, P], F32, tag="turned", name="sink_turned")
            nc.tensor.transpose(sink_turned[:, 0, :], sink_row[:], ident[:])
            nc.vector.tensor_scalar(neg_sink[:], sink_turned[:, 0, 0:1], -1.0, None, ALU.mult)
            nc.vector.tensor_scalar(sink_col[:], neg_sink[:], -1.0, None, ALU.mult)

        def token_scales():
            nc.vector.tensor_copy(vs_picked[:], listed(vs_pool, 0, N))
            for g in range(PASSES):
                vs_turned = turned_pool.tile([P, PACK, P], F32, tag="turned", name="vs_turned")
                for t in range(PACK):
                    nc.tensor.transpose(
                        vs_turned[:, t, :], vs_picked[:, g * PASS + t : (g + 1) * PASS : PACK], ident[:]
                    )
                nc.scalar.copy(vs_cols[:, g, :], vs_turned[:, :, 0])

        def keys(j, start=0, stop=N):
            nc.vector.tensor_copy(k_grouped[:, start:stop, j], listed(k_pool[j], start, stop))

        def scores(i):
            start, stop = PIECES[i]
            nc.vector.quantize_mx(
                out=k_codes[i][:].bitcast(FP8X4),
                scales=k_scales[i][:],
                in_=k_grouped[:, start:stop, :].rearrange("p s j -> p (s j)"),
            )
            nc.tensor.matmul_mx(
                out=score[i][:],
                lhsT=q_codes[:].bitcast(FP8X4),
                lhsT_scale=q_scales[:],
                rhs=k_codes[i][:].bitcast(FP8X4),
                rhs_scale=k_scales[i][:],
                start=True,
                stop=True,
            )
            nc.scalar.activation(capped[:, start:stop], score[i][:], ACT.Tanh, scale=0.5)

        def maxima(i):
            start, stop = PIECES[i]
            before = neg_sink if i == 0 else neg_max[i - 1]
            nc.vector.tensor_scalar(
                minus_capped[:, start:stop],
                capped[:, start:stop],
                -2.0,
                before[:],
                ALU.mult,
                ALU.min,
                accum_out=neg_max[i][:],
            )

        def exps(g):
            nc.scalar.activation(
                p[:, g].rearrange("q t s -> q s t"),
                capped[:, g * PASS : (g + 1) * PASS].rearrange("q (s t) -> q s t", t=PACK),
                ACT.Exp,
                bias=neg_max[-1][:],
                scale=2.0,
                accum_out=terms[:, g : g + 1],
            )

        def weights(g):
            p_turned = turned_pool.tile([P, PACK, P], F32, tag="turned", name="p_turned")
            for t in range(PACK):
                nc.tensor.transpose(p_turned[:, t, :], p[:, g, t, :], ident[:])
            w_grouped = shared1.tile([P, NQ, PACK], BF16, align_bytes=64, offset=g * NQ * PACK * 2, name=f"w_grouped{g}")
            nc.vector.tensor_tensor(
                w_grouped[:],
                p_turned[:].rearrange("p j q -> p q j"),
                vs_cols[:, g, :].unsqueeze(1).to_broadcast([P, NQ, PACK]),
                ALU.mult,
            )
            return w_grouped

        def weight_codes(g, w_grouped):
            nc.vector.quantize_mx(
                out=w_codes[g][:].bitcast(FP8X4),
                scales=w_scales[g][:],
                in_=w_grouped[:].rearrange("p q j -> p (q j)"),
            )

        def totals():
            nc.scalar.activation(terms[:, PASSES : PASSES + 1], sink_col[:], ACT.Exp, bias=neg_max[-1][:])
            nc.vector.reduce_sum(total[:], terms[:], mybir.AxisListType.X)
            nc.vector.reciprocal(recip[:], total[:])

        def values(b, g):
            picked = v1_picked[:, g].rearrange("p t s -> p s t") if b else v0_picked[:, g * PASS : (g + 1) * PASS]
            nc.vector.tensor_copy(picked, listed(v_pool[b], g * PASS, (g + 1) * PASS))

        def turn_values(b, g):
            v_turned = turned_pool.tile([P, PACK, P], BF16 if b else F32, tag="turned", name="v_turned")
            for t in range(PACK):
                if b:
                    nc.tensor.transpose(v_turned[:, t, :], v1_picked[:, g, t, :], ident_bf[:])
                else:
                    nc.tensor.transpose(v_turned[:, t, :], v0_picked[:, g * PASS + t : (g + 1) * PASS : PACK], ident[:])
            nc.scalar.copy(v_grouped[b][:, g], v_turned[:].rearrange("p j e -> p e j"))

        def value_codes(b, v_codes, first, last):
            nc.vector.quantize_mx(
                out=v_codes[:, first * P : last * P].bitcast(FP8X4),
                scales=v_scales[b][:, first * P : last * P],
                in_=v_grouped[b][:, first:last].rearrange("p g e j -> p (g e j)"),
            )

        def products(b, v_codes):
            y = sums_pool.tile([NQ, P], F32, name=f"y{b}")
            for g in range(PASSES):
                nc.tensor.matmul_mx(
                    out=y[:],
                    lhsT=w_codes[g][:].bitcast(FP8X4),
                    lhsT_scale=w_scales[g][:],
                    rhs=v_codes[:, g * P : (g + 1) * P].bitcast(FP8X4),
                    rhs_scale=v_scales[b][:, g * P : (g + 1) * P],
                    start=(g == 0),
                    stop=(g == PASSES - 1),
                )
            result(y, b * P, (b + 1) * P)

        def result(y, first, last):
            y_out = held.tile([NQ, last - first], F32, name=f"y_out{first}")
            nc.scalar.activation(y_out[:], y[:], ACT.Copy, scale=recip[:])
            nc.sync.dma_start(out[0, :, first:last], y_out[:])

        keys(0)
        queries()
        keys(1)
        sinks()
        token_scales()
        keys(2)
        keys(3, 0, 512)
        scores(0)
        keys(3, 512, 1024)
        scores(1)
        values(0, 0)
        values(0, 1)
        minus_capped = shared0.tile([NQ, N], F32, align_bytes=64, offset=0, name="minus_capped")
        maxima(0)
        maxima(1)
        exps(0)
        exps(1)
        values(1, 0)
        values(1, 1)
        w0 = weights(0)
        w1 = weights(1)
        turn_values(0, 0)
        turn_values(0, 1)
        turn_values(1, 0)
        turn_values(1, 1)
        weight_codes(0, w0)
        weight_codes(1, w1)
        total = shared1.tile([NQ, 1], F32, align_bytes=64, offset=2 * NQ * PACK * 2, name="total")
        totals()
        v_codes0 = held.tile([P, PASSES * P], U32, align_bytes=64, name="v_codes0")
        value_codes(0, v_codes0, 0, 2)
        v_codes1 = held.tile([P, PASSES * P], U32, align_bytes=64, name="v_codes1")
        value_codes(1, v_codes1, 0, 1)
        value_codes(1, v_codes1, 1, 2)
        products(0, v_codes0)
        products(1, v_codes1)
